import numpy as np
import ml_dtypes


def mxq(x, axis, fmt="e4m3"):
    dtype, down = {"e4m3": (ml_dtypes.float8_e4m3fn, 7), "e5m2": (ml_dtypes.float8_e5m2, 14)}[fmt]
    v = np.moveaxis(np.asarray(x, np.float32).astype(ml_dtypes.bfloat16).astype(np.float64), axis, -1)
    blocks = v.reshape(v.shape[:-1] + (-1, 32))
    amax = np.abs(blocks).max(-1, keepdims=True)
    byte = np.maximum(np.where(amax > 0, np.frexp(amax)[1] - 1 + 127, 0) - down, 1)
    scale = np.exp2(byte - 127.0)
    codes = (blocks / scale).astype(np.float32).astype(dtype).astype(np.float64)
    return np.moveaxis((codes * scale).reshape(v.shape), -1, axis)


WIDE = False


def mx_kscale(k):
    if not WIDE:
        return np.ones(k)
    levels = np.array([10, -10, 5, -5, 0])
    if k % 512:
        return np.exp2(np.random.permutation(np.resize(levels, k // 32))).repeat(32)
    a = np.empty((k // 512, 16))
    for p in range(k // 512):
        a[p, :8] = np.random.permutation(np.resize(levels, 8))
        for g in range(8):
            far = levels[np.abs(levels - a[p, g]) >= 10]
            a[p, g + 8] = far[np.random.randint(len(far))]
    return np.exp2(a.ravel()).repeat(32)


def f64(x):
    return np.asarray(x).astype(np.float64)


def striped(idx):
    return np.tile(idx.reshape(-1, 16).T, (8, 1)).astype(np.uint16)


def unstriped(offs):
    return offs[:16].T.reshape(-1).astype(np.int64)


def striped8(idx):
    return np.concatenate([x.reshape(-1, 16).T for x in idx]).astype(np.uint16)


def runs(offs, k):
    lists = np.stack([offs[16 * r : 16 * r + 16].T.reshape(-1) for r in range(8)]).astype(np.int64)
    return lists[np.arange(k) % 512 // 64]


def pack_weight(w):
    k, n = w.shape
    w = f64(np.asarray(w, np.float32).astype(ml_dtypes.bfloat16)).reshape(k // 32, 32, n)
    amax = np.abs(w).max(1)
    byte = np.clip(np.where(amax > 0, np.frexp(amax)[1] - 1 + 127 - 7, 1), 1, 254)
    scaled = (w * np.exp2(127.0 - byte)[:, None, :]).reshape(k, n).astype(np.float32)
    words = np.ascontiguousarray(scaled.reshape(k // 512, 128, 4, n).transpose(0, 1, 3, 2)).astype(ml_dtypes.float8_e4m3fn).view(np.uint8)
    return words, np.ascontiguousarray(byte.astype(np.uint8).reshape(k // 512, 16, n))


def unpack_weight(words, scales):
    g, p, n, _ = words.shape
    vals = np.ascontiguousarray(words).view(ml_dtypes.float8_e4m3fn).astype(np.float64) * np.repeat(np.exp2(scales.astype(np.float64) - 127.0), 8, axis=1)[..., None]
    return vals.transpose(0, 1, 3, 2).reshape(g * 512, n)


def relu(v):
    return np.maximum(v, 0.0)


def sigmoid(v):
    return 1.0 / (1.0 + np.exp(-np.maximum(v, -700.0)))

def planes(y):
    n, m = y.shape
    v = y.astype(np.float32).astype(ml_dtypes.bfloat16).astype(np.float64).reshape(n // 32, 32, m)
    top = np.abs(v).max(1)
    byte = np.clip(np.where(top > 0, np.frexp(top)[1] - 1 + 127 - 7, 1), 1, 254)
    codes = (v * np.exp2(127.0 - byte)[:, None, :]).reshape(n, m).astype(np.float32).astype(ml_dtypes.float8_e4m3fn).view(np.uint8)
    words = codes.reshape(n // 512, 128, 4, m).transpose(0, 1, 3, 2)
    return np.ascontiguousarray(words), np.ascontiguousarray(byte.astype(np.uint8).reshape(n // 512, 16, m))


K, T, S, G, H, C = 512, 1024, 256, 2048, 512, 512


def setup_inputs():
    n = np.random.standard_normal
    s = mx_kscale(K)[:, None]
    packed_xT = pack_weight(n((K, T)) * s)
    packed_dT = pack_weight(n((K, G)) / s)
    return {
        "x_words": packed_xT[0],
        "x_scales": packed_xT[1],
        "d_words": packed_dT[0],
        "d_scales": packed_dT[1],
        "gs": (np.random.uniform(0.5, 1.5, (K, 1)) / s).astype(np.float32),
        "offs": striped(np.random.permutation(T)[:S]),
        "k1": striped8(np.random.randint(0, G, (8, H))),
        "n1": striped(np.random.permutation(S)),
        "cand": striped(np.random.permutation(T)[:C]),
        "two": striped(np.random.permutation(T)[:S]),
        "k2": striped8(np.random.randint(0, G, (8, H))),
        "n2": striped(np.random.permutation(S)),
        "n3": striped(np.random.permutation(S)),
    }


def reference(x_words, x_scales, d_words, d_scales, gs, offs, k1, n1, cand, two, k2, n2, n3):
    x_cand = unpack_weight(x_words, x_scales)[:, unstriped(cand)]
    d_k1 = unpack_weight(d_words, d_scales)[np.arange(K)[:, None], runs(k1, K)]
    xq = unpack_weight(x_words, x_scales)[:, unstriped(offs)]
    h = 0.0625 * (d_k1.T @ xq)
    rl = relu(h)
    ds = np.zeros((H, S))
    ds[:, unstriped(n1)] = rl
    z = f64(gs) * (ds - (0.5 * h))
    a = 0.0625 * ((x_cand.T @ mxq(z, 0, "e4m3")))
    d_k2 = unpack_weight(d_words, d_scales)[np.arange(K)[:, None], runs(k2, K)]
    x_two = unpack_weight(x_words, x_scales)[:, unstriped(two)]
    b = 0.0625 * (d_k2.T @ x_two)
    out_0 = a + (sigmoid(b[:, unstriped(n3)] - b)) * (a[:, unstriped(n2)] - a)
    return (out_0,) + planes(out_0)

@@ -1,0 +1,203 @@
+from contextlib import ExitStack
+
+import concourse.mybir as mybir
+
+K, T, S, G, H, C = 512, 1024, 256, 2048, 512, 512
+FLOPS = 2 * K * S * (H + C + H)
+
+F32 = mybir.dt.float32
+BF16 = mybir.dt.bfloat16
+I32 = mybir.dt.int32
+U32 = mybir.dt.uint32
+U16 = mybir.dt.uint16
+U8 = mybir.dt.uint8
+FP8X4 = mybir.dt.float8_e4m3fn_x4
+ACT = mybir.ActivationFunctionType
+ALU = mybir.AluOpType
+
+P = 128
+PACK = 4
+QUAD = 32
+LIST_ROWS = 16
+
+
+def tile_picked_pqcjpullbsend_none_po_kernel(
+    tc, x_words, x_scales, d_words, d_scales, gs, offs, k1, n1, cand, two, k2, n2, n3, out_0, out_1, out_2
+):
+    nc = tc.nc
+    with ExitStack() as ctx:
+        lists = ctx.enter_context(tc.tile_pool(name="lists", bufs=1))
+        sb = ctx.enter_context(tc.tile_pool(name="sb", bufs=1))
+        psum = ctx.enter_context(tc.psum_pool(name="psum", bufs=1))
+
+        def load_list(src, name):
+            tile = lists.tile([P, src.shape[1]], U16, name=name)
+            nc.sync.dma_start(tile[:], src)
+            return tile
+
+        def new(shape, dtype, name, slot=None):
+            return sb.tile(shape, dtype, name=name, tag=slot or name, align_bytes=64)
+
+        d_byte_table = new([P, G], U8, "d_byte_table")
+        x_byte_table = new([P, T], U8, "x_byte_table")
+        d_word_table = new([P, G], U32, "d_word_table")
+        x_word_table = new([P, T], U32, "x_word_table")
+        gain = new([P, PACK], F32, "gain")
+
+        nc.gpsimd.dma_start(gain[:], gs.rearrange("(p t) one -> p (t one)", t=PACK))
+        nc.sync.dma_start(
+            d_byte_table[:].bitcast(I32), d_scales[0].bitcast(I32).unsqueeze(1).to_broadcast([16, 8, G // 4])
+        )
+        k1_list = load_list(k1, "k1_list")
+        offs_list = load_list(offs, "offs_list")
+        for q in range(P // QUAD):
+            nc.sync.dma_start(
+                x_byte_table[QUAD * q : QUAD * (q + 1), :].bitcast(I32),
+                x_scales[0][4 * q : 4 * q + 4, :].bitcast(I32).unsqueeze(0).to_broadcast([8, 4, T // 4]),
+            )
+        nc.sync.dma_start(d_word_table[:].bitcast(I32), d_words[0].rearrange("p c t -> p (c t)").bitcast(I32))
+        n1_list = load_list(n1, "n1_list")
+        k2_list = load_list(k2, "k2_list")
+        two_list = load_list(two, "two_list")
+        nc.sync.dma_start(x_word_table[:].bitcast(I32), x_words[0].rearrange("p c t -> p (c t)").bitcast(I32))
+        cand_list = load_list(cand, "cand_list")
+        n3_list = load_list(n3, "n3_list")
+        n2_list = load_list(n2, "n2_list")
+
+        def gather(table, offsets, width, dtype, name, slot=None):
+            picked = new([P, width], dtype, name, slot)
+            nc.vector.tensor_copy(picked[:], table[:].indirect(offsets[:]))
+            return picked
+
+        def gather_dealt(table, offsets, dtype, name, slot):
+            picked = new([P, PACK * P], dtype, name, slot)
+            nc.vector.tensor_copy(picked[:].rearrange("p (t m) -> p m t", t=PACK), table[:].indirect(offsets[:]))
+            return picked
+
+        def deal(picked, run, dtype, name):
+            dealt = new([P, PACK * P], dtype, name)
+            nc.vector.tensor_copy(
+                dealt[:].rearrange("p (t b i) -> p b t i", t=PACK, i=run),
+                picked[:].rearrange("p (b i t) -> p b t i", t=PACK, i=run),
+            )
+            return dealt
+
+        def coded_plane(picked, queue, name):
+            plane = deal(picked, 16, U8, name)
+            for j in range(1, 4):
+                queue.dma_start(plane[j:P:QUAD, :].bitcast(I32), plane[8 * j : P : QUAD, :].bitcast(I32))
+            return plane
+
+        def product(acc, t, words, plane, moving_words, moving_plane):
+            cols = slice(P * t, P * (t + 1))
+            nc.tensor.matmul_mx(
+                out=acc,
+                lhsT=words[:, cols].bitcast(FP8X4),
+                lhsT_scale=plane[:, cols],
+                rhs=moving_words[:].bitcast(FP8X4),
+                rhs_scale=moving_plane[:],
+                start=True,
+                stop=True,
+            )
+
+        def interleave(src, name):
+            grouped = new([P, S, PACK], BF16, name)
+            nc.vector.tensor_copy(
+                grouped[:].rearrange("p (c i) t -> p c t i", i=4), src[:].rearrange("p t (c i) -> p c t i", i=4)
+            )
+            return grouped
+
+        def quantise(grouped, name, slot=None):
+            words = new([P, S], U32, name + "_words", slot)
+            plane = new([P, S], U8, name + "_plane")
+            nc.vector.quantize_mx(
+                out=words[:].bitcast(FP8X4), scales=plane[:], in_=grouped[:].rearrange("p c t -> p (c t)")
+            )
+            return words, plane
+
+        gain_pos = new([P, PACK], F32, "gain_pos")
+        gain_neg = new([P, PACK], F32, "gain_neg")
+        nc.scalar.activation(gain_pos[:], gain[:], ACT.Copy, scale=0.0625)
+        nc.scalar.activation(gain_neg[:], gain[:], ACT.Copy, scale=-0.03125)
+
+        d1_plane = coded_plane(gather(d_byte_table, k1_list, H, U8, "d1_bytes"), nc.scalar, "d1_plane")
+        xq_plane = gather(x_byte_table, offs_list, S, U8, "xq_plane", "d1_bytes")
+        d1_picked = gather(d_word_table, k1_list, H, U32, "d1_picked")
+        xq_words = gather(x_word_table, offs_list, S, U32, "xq_words")
+        d1_words = deal(d1_picked, 4, U32, "d1_words")
+        h_banks = [psum.tile([P, 2, S], F32, name="h_bank%d" % u) for u in range(2)]
+        h_acc = [h_banks[t // 2][:, t % 2, :] for t in range(PACK)]
+        for t in range(PACK):
+            product(h_acc[t], t, d1_words, d1_plane, xq_words, xq_plane)
+
+        rows = new([P, 9 * S], F32, "rows")
+        sent = []
+
+        def send(t):
+            positive = rows[:, 8 * S : 9 * S] if t == 0 else new([P, S], F32, "positive%d" % t)[:]
+            nc.vector.tensor_scalar(positive, h_acc[t], 0.0, gain_pos[:, t : t + 1], ALU.max, ALU.mult)
+            window = new([P, 2 * S], F32, "sent%d" % t)
+            nc.scalar.activation(window[:].indirect(n1_list[:]), positive, ACT.Copy)
+            sent.append(window)
+
+        send(0)
+        send(1)
+        d2_bytes = gather(d_byte_table, k2_list, H, U8, "d2_bytes", "d1_bytes")
+        send(2)
+        d2_plane = coded_plane(d2_bytes, nc.sync, "d2_plane")
+        send(3)
+        d2_picked = gather(d_word_table, k2_list, H, U32, "d2_picked", "d1_words")
+        x2_plane = gather(x_byte_table, two_list, S, U8, "x2_plane", "gain_pos")
+        d2_words = deal(d2_picked, 4, U32, "d2_words")
+        x2_words = gather(x_word_table, two_list, S, U32, "x2_words", "xq_words")
+        b_banks = [psum.tile([P, 2, S], F32, name="b_bank%d" % u) for u in range(2)]
+        for t in reversed(range(PACK)):
+            product(b_banks[t // 2][:, t % 2, :], t, d2_words, d2_plane, x2_words, x2_plane)
+        xc_plane = gather_dealt(x_byte_table, cand_list, U8, "xc_plane", "d1_plane")
+        xc_words = gather_dealt(x_word_table, cand_list, U32, "xc_words", "d1_words")
+
+        z_rows = new([P, PACK, S], BF16, "z_rows")
+        for t in range(PACK):
+            nc.vector.scalar_tensor_tensor(
+                z_rows[:, t, :], h_acc[t], gain_neg[:, t : t + 1], sent[t][:, 0:S], ALU.mult, ALU.add
+            )
+        z_words, z_plane = quantise(interleave(z_rows, "z_grouped"), "z", "xq_words")
+        a_acc = [psum.tile([P, S], F32, name="a_bank%d" % t) for t in range(PACK)]
+        for t in reversed(range(PACK)):
+            product(a_acc[t][:], t, xc_words, xc_plane, z_words, z_plane)
+
+        b_far = new([P, PACK * S], F32, "b_far")
+        for u in reversed(range(2)):
+            lo = S * (PACK + 2 * u)
+            nc.scalar.activation(rows[:, lo : lo + 2 * S], b_banks[u][:].rearrange("p e c -> p (e c)"), ACT.Copy)
+            for t in (2 * u + 1, 2 * u):
+                lo = S * (PACK + t)
+                nc.scalar.activation(b_far[:, S * t : S * (t + 1)], rows[:, lo : lo + 2 * S].indirect(n3_list[:]), ACT.Copy)
+        gap = new([P, PACK * S], F32, "gap", "z_grouped")
+        for u in reversed(range(2)):
+            pair = slice(2 * S * u, 2 * S * (u + 1))
+            nc.vector.tensor_tensor(gap[:, pair], b_far[:, pair], b_banks[u][:].rearrange("p e c -> p (e c)"), ALU.subtract)
+
+        gate = new([P, PACK * S], F32, "gate")
+        result = new([P, PACK, S], F32, "result")
+        out_rows = out_0.rearrange("(p t) c -> p t c", t=PACK)
+        for t in reversed(range(PACK)):
+            own = slice(S * t, S * (t + 1))
+            nc.scalar.activation(rows[:, own], a_acc[t][:], ACT.Copy, scale=0.03125)
+            if t % 2:
+                pair = slice(S * (t - 1), S * (t + 1))
+                nc.scalar.activation(gate[:, pair], gap[:, pair], ACT.Tanh, scale=0.03125)
+            far = new([P, S], F32, "a_far%d" % t)
+            nc.scalar.activation(far[:], rows[:, S * t : S * (t + 2)].indirect(n2_list[:]), ACT.Copy)
+            near_part = new([P, S], F32, "near_part%d" % t)
+            nc.vector.scalar_tensor_tensor(near_part[:], gate[:, own], 1.0, rows[:, own], ALU.subtract, ALU.mult)
+            far_part = new([P, S], F32, "far_part%d" % t)
+            nc.vector.scalar_tensor_tensor(far_part[:], gate[:, own], 1.0, far[:], ALU.add, ALU.mult)
+            nc.vector.tensor_tensor(result[:, t, :], far_part[:], near_part[:], ALU.subtract)
+            nc.sync.dma_start(out_rows[:, t, :], result[:, t, :])
+
+        y_words, y_plane = quantise(interleave(result, "y_grouped"), "y")
+        nc.sync.dma_start(out_1[0].rearrange("p c t -> p (c t)").bitcast(I32), y_words[:].bitcast(I32))
+        for q in range(P // QUAD):
+            queue = nc.scalar if q % 2 else nc.sync
+            queue.dma_start(out_2[0][4 * q : 4 * q + 4, :].bitcast(I32), y_plane[QUAD * q : QUAD * q + 4, :].bitcast(I32))

@@ -44,7 +44,6 @@ def tile_picked_pqcjpullbsend_none_po_kernel(
         x_word_table = new([P, T], U32, "x_word_table")
         gain = new([P, PACK], F32, "gain")
 
-        nc.gpsimd.dma_start(gain[:], gs.rearrange("(p t) one -> p (t one)", t=PACK))
         nc.sync.dma_start(
             d_byte_table[:].bitcast(I32), d_scales[0].bitcast(I32).unsqueeze(1).to_broadcast([16, 8, G // 4])
         )
@@ -56,10 +55,11 @@ def tile_picked_pqcjpullbsend_none_po_kernel(
                 x_scales[0][4 * q : 4 * q + 4, :].bitcast(I32).unsqueeze(0).to_broadcast([8, 4, T // 4]),
             )
         nc.sync.dma_start(d_word_table[:].bitcast(I32), d_words[0].rearrange("p c t -> p (c t)").bitcast(I32))
+        nc.sync.dma_start(gain[:], gs.rearrange("(p t) one -> p (t one)", t=PACK))
         n1_list = load_list(n1, "n1_list")
         k2_list = load_list(k2, "k2_list")
-        two_list = load_list(two, "two_list")
         nc.sync.dma_start(x_word_table[:].bitcast(I32), x_words[0].rearrange("p c t -> p (c t)").bitcast(I32))
+        two_list = load_list(two, "two_list")
         cand_list = load_list(cand, "cand_list")
         n3_list = load_list(n3, "n3_list")
         n2_list = load_list(n2, "n2_list")
@@ -100,19 +100,23 @@ def tile_picked_pqcjpullbsend_none_po_kernel(
                 stop=True,
             )
 
-        def interleave(src, name):
-            grouped = new([P, S, PACK], BF16, name)
-            nc.vector.tensor_copy(
-                grouped[:].rearrange("p (c i) t -> p c t i", i=4), src[:].rearrange("p t (c i) -> p c t i", i=4)
+        halves = [slice(0, S // 2), slice(S // 2, S)]
+
+        def regroup(copy, grouped, src, cols, tiles):
+            copy(
+                grouped[:, cols, tiles].rearrange("p (c i) t -> p c t i", i=4),
+                src[:, tiles, cols].rearrange("p t (c i) -> p c t i", i=4),
             )
-            return grouped
 
         def quantise(grouped, name, slot=None):
             words = new([P, S], U32, name + "_words", slot)
             plane = new([P, S], U8, name + "_plane")
-            nc.vector.quantize_mx(
-                out=words[:].bitcast(FP8X4), scales=plane[:], in_=grouped[:].rearrange("p c t -> p (c t)")
-            )
+            for half in halves:
+                nc.vector.quantize_mx(
+                    out=words[:, half].bitcast(FP8X4),
+                    scales=plane[:, half],
+                    in_=grouped[:, half, :].rearrange("p c t -> p (c t)"),
+                )
             return words, plane
 
         gain_pos = new([P, PACK], F32, "gain_pos")
@@ -123,10 +127,10 @@ def tile_picked_pqcjpullbsend_none_po_kernel(
         d1_plane = coded_plane(gather(d_byte_table, k1_list, H, U8, "d1_bytes"), nc.scalar, "d1_plane")
         xq_plane = gather(x_byte_table, offs_list, S, U8, "xq_plane", "d1_bytes")
         d1_picked = gather(d_word_table, k1_list, H, U32, "d1_picked")
-        xq_words = gather(x_word_table, offs_list, S, U32, "xq_words")
         d1_words = deal(d1_picked, 4, U32, "d1_words")
-        h_banks = [psum.tile([P, 2, S], F32, name="h_bank%d" % u) for u in range(2)]
-        h_acc = [h_banks[t // 2][:, t % 2, :] for t in range(PACK)]
+        xq_words = gather(x_word_table, offs_list, S, U32, "xq_words")
+        x2_plane = gather(x_byte_table, two_list, S, U8, "x2_plane", "d1_picked")
+        h_acc = [psum.tile([P, S], F32, name="h_acc%d" % t, tag="bank%d" % t)[:] for t in range(PACK)]
         for t in range(PACK):
             product(h_acc[t], t, d1_words, d1_plane, xq_words, xq_plane)
 
@@ -147,9 +151,8 @@ def tile_picked_pqcjpullbsend_none_po_kernel(
         d2_plane = coded_plane(d2_bytes, nc.sync, "d2_plane")
         send(3)
         d2_picked = gather(d_word_table, k2_list, H, U32, "d2_picked", "d1_words")
-        x2_plane = gather(x_byte_table, two_list, S, U8, "x2_plane", "gain_pos")
-        d2_words = deal(d2_picked, 4, U32, "d2_words")
         x2_words = gather(x_word_table, two_list, S, U32, "x2_words", "xq_words")
+        d2_words = deal(d2_picked, 4, U32, "d2_words")
         b_banks = [psum.tile([P, 2, S], F32, name="b_bank%d" % u) for u in range(2)]
         for t in reversed(range(PACK)):
             product(b_banks[t // 2][:, t % 2, :], t, d2_words, d2_plane, x2_words, x2_plane)
@@ -161,42 +164,60 @@ def tile_picked_pqcjpullbsend_none_po_kernel(
             nc.vector.scalar_tensor_tensor(
                 z_rows[:, t, :], h_acc[t], gain_neg[:, t : t + 1], sent[t][:, 0:S], ALU.mult, ALU.add
             )
-        z_words, z_plane = quantise(interleave(z_rows, "z_grouped"), "z", "xq_words")
-        a_acc = [psum.tile([P, S], F32, name="a_bank%d" % t) for t in range(PACK)]
+        z_grouped = new([P, S, PACK], BF16, "z_grouped")
+        for half in halves:
+            regroup(nc.vector.tensor_copy, z_grouped, z_rows, half, slice(0, PACK))
+        z_words, z_plane = quantise(z_grouped, "z", "xq_words")
+        a_acc = [psum.tile([P, S], F32, name="a_acc%d" % t, tag="bank%d" % t) for t in range(PACK)]
         for t in reversed(range(PACK)):
             product(a_acc[t][:], t, xc_words, xc_plane, z_words, z_plane)
 
         b_far = new([P, PACK * S], F32, "b_far")
+        gaps = [new([P, 2 * S], F32, "gap%d" % u) for u in range(2)]
         for u in reversed(range(2)):
             lo = S * (PACK + 2 * u)
             nc.scalar.activation(rows[:, lo : lo + 2 * S], b_banks[u][:].rearrange("p e c -> p (e c)"), ACT.Copy)
             for t in (2 * u + 1, 2 * u):
                 lo = S * (PACK + t)
                 nc.scalar.activation(b_far[:, S * t : S * (t + 1)], rows[:, lo : lo + 2 * S].indirect(n3_list[:]), ACT.Copy)
-        gap = new([P, PACK * S], F32, "gap", "z_grouped")
-        for u in reversed(range(2)):
-            pair = slice(2 * S * u, 2 * S * (u + 1))
-            nc.vector.tensor_tensor(gap[:, pair], b_far[:, pair], b_banks[u][:].rearrange("p e c -> p (e c)"), ALU.subtract)
+                nc.gpsimd.tensor_tensor(
+                    gaps[u][:, S * (t % 2) : S * (t % 2 + 1)],
+                    b_far[:, S * t : S * (t + 1)],
+                    rows[:, lo : lo + S],
+                    ALU.subtract,
+                )
 
         gate = new([P, PACK * S], F32, "gate")
         result = new([P, PACK, S], F32, "result")
         out_rows = out_0.rearrange("(p t) c -> p t c", t=PACK)
         for t in reversed(range(PACK)):
             own = slice(S * t, S * (t + 1))
-            nc.scalar.activation(rows[:, own], a_acc[t][:], ACT.Copy, scale=0.03125)
+            nc.vector.tensor_scalar(rows[:, own], a_acc[t][:], 0.03125, None, ALU.mult)
             if t % 2:
-                pair = slice(S * (t - 1), S * (t + 1))
-                nc.scalar.activation(gate[:, pair], gap[:, pair], ACT.Tanh, scale=0.03125)
-            far = new([P, S], F32, "a_far%d" % t)
-            nc.scalar.activation(far[:], rows[:, S * t : S * (t + 2)].indirect(n2_list[:]), ACT.Copy)
+                nc.scalar.activation(gate[:, S * (t - 1) : S * (t + 1)], gaps[t // 2][:], ACT.Tanh, scale=0.03125)
+            far = new([P, S], F32, "a_far%d" % t, "gap%d" % (t // 2) if t % 2 else None)
             near_part = new([P, S], F32, "near_part%d" % t)
-            nc.vector.scalar_tensor_tensor(near_part[:], gate[:, own], 1.0, rows[:, own], ALU.subtract, ALU.mult)
             far_part = new([P, S], F32, "far_part%d" % t)
-            nc.vector.scalar_tensor_tensor(far_part[:], gate[:, own], 1.0, far[:], ALU.add, ALU.mult)
-            nc.vector.tensor_tensor(result[:, t, :], far_part[:], near_part[:], ALU.subtract)
+            pieces = halves if t == 0 else [slice(0, S)]
+            for piece in pieces:
+                entries = n2_list[:, piece.start // LIST_ROWS : piece.stop // LIST_ROWS]
+                nc.scalar.activation(far[:, piece], rows[:, S * t : S * (t + 2)].indirect(entries), ACT.Copy)
+            nc.vector.scalar_tensor_tensor(near_part[:], gate[:, own], 1.0, a_acc[t][:], ALU.subtract, ALU.mult)
+            for piece in pieces:
+                nc.vector.scalar_tensor_tensor(
+                    far_part[:, piece], gate[:, own][:, piece], 1.0, far[:, piece], ALU.add, ALU.mult
+                )
+            for piece in pieces:
+                nc.vector.scalar_tensor_tensor(
+                    result[:, t, piece], near_part[:, piece], -0.03125, far_part[:, piece], ALU.mult, ALU.add
+                )
             nc.sync.dma_start(out_rows[:, t, :], result[:, t, :])
 
-        y_words, y_plane = quantise(interleave(result, "y_grouped"), "y")
+        y_grouped = new([P, S, PACK], BF16, "y_grouped", "gap0")
+        regroup(nc.scalar.copy, y_grouped, result, slice(0, S), slice(2, PACK))
+        for half in halves:
+            regroup(nc.vector.tensor_copy, y_grouped, result, half, slice(0, 2))
+        y_words, y_plane = quantise(y_grouped, "y")
         nc.sync.dma_start(out_1[0].rearrange("p c t -> p (c t)").bitcast(I32), y_words[:].bitcast(I32))
         for q in range(P // QUAD):
             queue = nc.scalar if q % 2 else nc.sync

@@ -130,6 +130,7 @@ def tile_picked_pqcjpullbsend_none_po_kernel(
         d1_words = deal(d1_picked, 4, U32, "d1_words")
         xq_words = gather(x_word_table, offs_list, S, U32, "xq_words")
         x2_plane = gather(x_byte_table, two_list, S, U8, "x2_plane", "d1_picked")
+        x2_words = gather(x_word_table, two_list, S, U32, "x2_words")
         h_acc = [psum.tile([P, S], F32, name="h_acc%d" % t, tag="bank%d" % t)[:] for t in range(PACK)]
         for t in range(PACK):
             product(h_acc[t], t, d1_words, d1_plane, xq_words, xq_plane)
@@ -151,7 +152,6 @@ def tile_picked_pqcjpullbsend_none_po_kernel(
         d2_plane = coded_plane(d2_bytes, nc.sync, "d2_plane")
         send(3)
         d2_picked = gather(d_word_table, k2_list, H, U32, "d2_picked", "d1_words")
-        x2_words = gather(x_word_table, two_list, S, U32, "x2_words", "xq_words")
         d2_words = deal(d2_picked, 4, U32, "d2_words")
         b_banks = [psum.tile([P, 2, S], F32, name="b_bank%d" % u) for u in range(2)]
         for t in reversed(range(PACK)):
@@ -167,7 +167,7 @@ def tile_picked_pqcjpullbsend_none_po_kernel(
         z_grouped = new([P, S, PACK], BF16, "z_grouped")
         for half in halves:
             regroup(nc.vector.tensor_copy, z_grouped, z_rows, half, slice(0, PACK))
-        z_words, z_plane = quantise(z_grouped, "z", "xq_words")
+        z_words, z_plane = quantise(z_grouped, "z", "x2_words")
         a_acc = [psum.tile([P, S], F32, name="a_acc%d" % t, tag="bank%d" % t) for t in range(PACK)]
         for t in reversed(range(PACK)):
             product(a_acc[t][:], t, xc_words, xc_plane, z_words, z_plane)
@@ -213,7 +213,7 @@ def tile_picked_pqcjpullbsend_none_po_kernel(
                 )
             nc.sync.dma_start(out_rows[:, t, :], result[:, t, :])
 
-        y_grouped = new([P, S, PACK], BF16, "y_grouped", "gap0")
+        y_grouped = new([P, S, PACK], BF16, "y_grouped", "rows")
         regroup(nc.scalar.copy, y_grouped, result, slice(0, S), slice(2, PACK))
         for half in halves:
             regroup(nc.vector.tensor_copy, y_grouped, result, half, slice(0, 2))

from contextlib import ExitStack

import concourse.mybir as mybir

K, T, S, G, H, C = 512, 1024, 256, 2048, 512, 512
FLOPS = 2 * K * S * (H + C + H)

F32 = mybir.dt.float32
BF16 = mybir.dt.bfloat16
I32 = mybir.dt.int32
U32 = mybir.dt.uint32
U16 = mybir.dt.uint16
U8 = mybir.dt.uint8
FP8X4 = mybir.dt.float8_e4m3fn_x4
ACT = mybir.ActivationFunctionType
ALU = mybir.AluOpType

P = 128
PACK = 4
QUAD = 32
LIST_ROWS = 16


def tile_picked_pqcjpullbsend_none_po_kernel(
    tc, x_words, x_scales, d_words, d_scales, gs, offs, k1, n1, cand, two, k2, n2, n3, out_0, out_1, out_2
):
    nc = tc.nc
    with ExitStack() as ctx:
        lists = ctx.enter_context(tc.tile_pool(name="lists", bufs=1))
        sb = ctx.enter_context(tc.tile_pool(name="sb", bufs=1))
        psum = ctx.enter_context(tc.psum_pool(name="psum", bufs=1))

        def load_list(src, name):
            tile = lists.tile([P, src.shape[1]], U16, name=name)
            nc.sync.dma_start(tile[:], src)
            return tile

        def new(shape, dtype, name, slot=None):
            return sb.tile(shape, dtype, name=name, tag=slot or name, align_bytes=64)

        d_byte_table = new([P, G], U8, "d_byte_table")
        x_byte_table = new([P, T], U8, "x_byte_table")
        d_word_table = new([P, G], U32, "d_word_table")
        x_word_table = new([P, T], U32, "x_word_table")
        gain = new([P, PACK], F32, "gain")

        nc.sync.dma_start(
            d_byte_table[:].bitcast(I32), d_scales[0].bitcast(I32).unsqueeze(1).to_broadcast([16, 8, G // 4])
        )
        k1_list = load_list(k1, "k1_list")
        offs_list = load_list(offs, "offs_list")
        for q in range(P // QUAD):
            nc.sync.dma_start(
                x_byte_table[QUAD * q : QUAD * (q + 1), :].bitcast(I32),
                x_scales[0][4 * q : 4 * q + 4, :].bitcast(I32).unsqueeze(0).to_broadcast([8, 4, T // 4]),
            )
        nc.sync.dma_start(d_word_table[:].bitcast(I32), d_words[0].rearrange("p c t -> p (c t)").bitcast(I32))
        nc.sync.dma_start(gain[:], gs.rearrange("(p t) one -> p (t one)", t=PACK))
        n1_list = load_list(n1, "n1_list")
        k2_list = load_list(k2, "k2_list")
        nc.sync.dma_start(x_word_table[:].bitcast(I32), x_words[0].rearrange("p c t -> p (c t)").bitcast(I32))
        two_list = load_list(two, "two_list")
        cand_list = load_list(cand, "cand_list")
        n3_list = load_list(n3, "n3_list")
        n2_list = load_list(n2, "n2_list")

        def gather(table, offsets, width, dtype, name, slot=None):
            picked = new([P, width], dtype, name, slot)
            nc.vector.tensor_copy(picked[:], table[:].indirect(offsets[:]))
            return picked

        def gather_dealt(table, offsets, dtype, name, slot):
            picked = new([P, PACK * P], dtype, name, slot)
            nc.vector.tensor_copy(picked[:].rearrange("p (t m) -> p m t", t=PACK), table[:].indirect(offsets[:]))
            return picked

        def deal(picked, run, dtype, name):
            dealt = new([P, PACK * P], dtype, name)
            nc.vector.tensor_copy(
                dealt[:].rearrange("p (t b i) -> p b t i", t=PACK, i=run),
                picked[:].rearrange("p (b i t) -> p b t i", t=PACK, i=run),
            )
            return dealt

        def coded_plane(picked, queue, name):
            plane = deal(picked, 16, U8, name)
            for j in range(1, 4):
                queue.dma_start(plane[j:P:QUAD, :].bitcast(I32), plane[8 * j : P : QUAD, :].bitcast(I32))
            return plane

        def product(acc, t, words, plane, moving_words, moving_plane):
            cols = slice(P * t, P * (t + 1))
            nc.tensor.matmul_mx(
                out=acc,
                lhsT=words[:, cols].bitcast(FP8X4),
                lhsT_scale=plane[:, cols],
                rhs=moving_words[:].bitcast(FP8X4),
                rhs_scale=moving_plane[:],
                start=True,
                stop=True,
            )

        halves = [slice(0, S // 2), slice(S // 2, S)]

        def regroup(copy, grouped, src, cols, tiles):
            copy(
                grouped[:, cols, tiles].rearrange("p (c i) t -> p c t i", i=4),
                src[:, tiles, cols].rearrange("p t (c i) -> p c t i", i=4),
            )

        def quantise(grouped, name, slot=None):
            words = new([P, S], U32, name + "_words", slot)
            plane = new([P, S], U8, name + "_plane")
            for half in halves:
                nc.vector.quantize_mx(
                    out=words[:, half].bitcast(FP8X4),
                    scales=plane[:, half],
                    in_=grouped[:, half, :].rearrange("p c t -> p (c t)"),
                )
            return words, plane

        gain_pos = new([P, PACK], F32, "gain_pos")
        gain_neg = new([P, PACK], F32, "gain_neg")
        nc.scalar.activation(gain_pos[:], gain[:], ACT.Copy, scale=0.0625)
        nc.scalar.activation(gain_neg[:], gain[:], ACT.Copy, scale=-0.03125)

        d1_plane = coded_plane(gather(d_byte_table, k1_list, H, U8, "d1_bytes"), nc.scalar, "d1_plane")
        xq_plane = gather(x_byte_table, offs_list, S, U8, "xq_plane", "d1_bytes")
        d1_picked = gather(d_word_table, k1_list, H, U32, "d1_picked")
        d1_words = deal(d1_picked, 4, U32, "d1_words")
        xq_words = gather(x_word_table, offs_list, S, U32, "xq_words")
        x2_plane = gather(x_byte_table, two_list, S, U8, "x2_plane", "d1_picked")
        x2_words = gather(x_word_table, two_list, S, U32, "x2_words")
        h_acc = [psum.tile([P, S], F32, name="h_acc%d" % t, tag="bank%d" % t)[:] for t in range(PACK)]
        for t in range(PACK):
            product(h_acc[t], t, d1_words, d1_plane, xq_words, xq_plane)

        rows = new([P, 9 * S], F32, "rows")
        sent = []

        def send(t):
            positive = rows[:, 8 * S : 9 * S] if t == 0 else new([P, S], F32, "positive%d" % t)[:]
            nc.vector.tensor_scalar(positive, h_acc[t], 0.0, gain_pos[:, t : t + 1], ALU.max, ALU.mult)
            window = new([P, 2 * S], F32, "sent%d" % t)
            nc.scalar.activation(window[:].indirect(n1_list[:]), positive, ACT.Copy)
            sent.append(window)

        send(0)
        send(1)
        d2_bytes = gather(d_byte_table, k2_list, H, U8, "d2_bytes", "d1_bytes")
        send(2)
        d2_plane = coded_plane(d2_bytes, nc.sync, "d2_plane")
        send(3)
        d2_picked = gather(d_word_table, k2_list, H, U32, "d2_picked", "d1_words")
        d2_words = deal(d2_picked, 4, U32, "d2_words")
        b_banks = [psum.tile([P, 2, S], F32, name="b_bank%d" % u) for u in range(2)]
        for t in reversed(range(PACK)):
            product(b_banks[t // 2][:, t % 2, :], t, d2_words, d2_plane, x2_words, x2_plane)
        xc_plane = gather_dealt(x_byte_table, cand_list, U8, "xc_plane", "d1_plane")
        xc_words = gather_dealt(x_word_table, cand_list, U32, "xc_words", "d1_words")

        z_rows = new([P, PACK, S], BF16, "z_rows")
        for t in range(PACK):
            nc.vector.scalar_tensor_tensor(
                z_rows[:, t, :], h_acc[t], gain_neg[:, t : t + 1], sent[t][:, 0:S], ALU.mult, ALU.add
            )
        z_grouped = new([P, S, PACK], BF16, "z_grouped")
        for half in halves:
            regroup(nc.vector.tensor_copy, z_grouped, z_rows, half, slice(0, PACK))
        z_words, z_plane = quantise(z_grouped, "z", "x2_words")
        a_acc = [psum.tile([P, S], F32, name="a_acc%d" % t, tag="bank%d" % t) for t in range(PACK)]
        for t in reversed(range(PACK)):
            product(a_acc[t][:], t, xc_words, xc_plane, z_words, z_plane)

        b_far = new([P, PACK * S], F32, "b_far")
        gaps = [new([P, 2 * S], F32, "gap%d" % u) for u in range(2)]
        for u in reversed(range(2)):
            lo = S * (PACK + 2 * u)
            nc.scalar.activation(rows[:, lo : lo + 2 * S], b_banks[u][:].rearrange("p e c -> p (e c)"), ACT.Copy)
            for t in (2 * u + 1, 2 * u):
                lo = S * (PACK + t)
                nc.scalar.activation(b_far[:, S * t : S * (t + 1)], rows[:, lo : lo + 2 * S].indirect(n3_list[:]), ACT.Copy)
                nc.gpsimd.tensor_tensor(
                    gaps[u][:, S * (t % 2) : S * (t % 2 + 1)],
                    b_far[:, S * t : S * (t + 1)],
                    rows[:, lo : lo + S],
                    ALU.subtract,
                )

        gate = new([P, PACK * S], F32, "gate")
        result = new([P, PACK, S], F32, "result")
        out_rows = out_0.rearrange("(p t) c -> p t c", t=PACK)
        for t in reversed(range(PACK)):
            own = slice(S * t, S * (t + 1))
            nc.vector.tensor_scalar(rows[:, own], a_acc[t][:], 0.03125, None, ALU.mult)
            if t % 2:
                nc.scalar.activation(gate[:, S * (t - 1) : S * (t + 1)], gaps[t // 2][:], ACT.Tanh, scale=0.03125)
            far = new([P, S], F32, "a_far%d" % t, "gap%d" % (t // 2) if t % 2 else None)
            near_part = new([P, S], F32, "near_part%d" % t)
            far_part = new([P, S], F32, "far_part%d" % t)
            pieces = halves if t == 0 else [slice(0, S)]
            for piece in pieces:
                entries = n2_list[:, piece.start // LIST_ROWS : piece.stop // LIST_ROWS]
                nc.scalar.activation(far[:, piece], rows[:, S * t : S * (t + 2)].indirect(entries), ACT.Copy)
            nc.vector.scalar_tensor_tensor(near_part[:], gate[:, own], 1.0, a_acc[t][:], ALU.subtract, ALU.mult)
            for piece in pieces:
                nc.vector.scalar_tensor_tensor(
                    far_part[:, piece], gate[:, own][:, piece], 1.0, far[:, piece], ALU.add, ALU.mult
                )
            for piece in pieces:
                nc.vector.scalar_tensor_tensor(
                    result[:, t, piece], near_part[:, piece], -0.03125, far_part[:, piece], ALU.mult, ALU.add
                )
            nc.sync.dma_start(out_rows[:, t, :], result[:, t, :])

        y_grouped = new([P, S, PACK], BF16, "y_grouped", "rows")
        regroup(nc.scalar.copy, y_grouped, result, slice(0, S), slice(2, PACK))
        for half in halves:
            regroup(nc.vector.tensor_copy, y_grouped, result, half, slice(0, 2))
        y_words, y_plane = quantise(y_grouped, "y")
        nc.sync.dma_start(out_1[0].rearrange("p c t -> p (c t)").bitcast(I32), y_words[:].bitcast(I32))
        for q in range(P // QUAD):
            queue = nc.scalar if q % 2 else nc.sync
            queue.dma_start(out_2[0][4 * q : 4 * q + 4, :].bitcast(I32), y_plane[QUAD * q : QUAD * q + 4, :].bitcast(I32))
